import numpy as np
import ml_dtypes


def mxq(x, axis, fmt="e4m3"):
    dtype, down = {"e4m3": (ml_dtypes.float8_e4m3fn, 7), "e5m2": (ml_dtypes.float8_e5m2, 14)}[fmt]
    v = np.moveaxis(np.asarray(x, np.float32).astype(ml_dtypes.bfloat16).astype(np.float64), axis, -1)
    blocks = v.reshape(v.shape[:-1] + (-1, 32))
    amax = np.abs(blocks).max(-1, keepdims=True)
    byte = np.maximum(np.where(amax > 0, np.frexp(amax)[1] - 1 + 127, 0) - down, 1)
    scale = np.exp2(byte - 127.0)
    codes = (blocks / scale).astype(np.float32).astype(dtype).astype(np.float64)
    return np.moveaxis((codes * scale).reshape(v.shape), -1, axis)


WIDE = False


def mx_kscale(k):
    if not WIDE:
        return np.ones(k)
    levels = np.array([10, -10, 5, -5, 0])
    if k % 512:
        return np.exp2(np.random.permutation(np.resize(levels, k // 32))).repeat(32)
    a = np.empty((k // 512, 16))
    for p in range(k // 512):
        a[p, :8] = np.random.permutation(np.resize(levels, 8))
        for g in range(8):
            far = levels[np.abs(levels - a[p, g]) >= 10]
            a[p, g + 8] = far[np.random.randint(len(far))]
    return np.exp2(a.ravel()).repeat(32)


def f64(x):
    return np.asarray(x).astype(np.float64)


def striped(idx):
    return np.tile(idx.reshape(-1, 16).T, (8, 1)).astype(np.uint16)


def unstriped(offs):
    return offs[:16].T.reshape(-1).astype(np.int64)


E2M1 = np.array([0.0, 0.5, 1.0, 1.5, 2.0, 3.0, 4.0, 6.0, -0.0, -0.5, -1.0, -1.5, -2.0, -3.0, -4.0, -6.0])


def pack_weight(w, fmt):
    k, n = w.shape
    w = f64(np.asarray(w, np.float32).astype(ml_dtypes.bfloat16)).reshape(k // 32, 32, n)
    amax = np.abs(w).max(1)
    if fmt == "e4m3":
        byte = np.frexp(amax)[1] - 1 + 127 - 7
    else:
        mant, ex = np.frexp(amax / 6.0)
        byte = np.where(mant > 0.5, ex, ex - 1) + 127
    byte = np.clip(np.where(amax > 0, byte, 1), 1, 254)
    scaled = (w * np.exp2(127.0 - byte)[:, None, :]).reshape(k, n).astype(np.float32)
    by_word = np.ascontiguousarray(scaled.reshape(k // 512, 128, 4, n).transpose(0, 1, 3, 2))
    if fmt == "e4m3":
        words = by_word.astype(ml_dtypes.float8_e4m3fn).view(np.uint8)
    else:
        c = by_word.astype(ml_dtypes.float4_e2m1fn).view(np.uint8) & 0xF
        words = (c[..., 0::2] | (c[..., 1::2] << 4)).reshape(k // 512, 128, 2 * n)
    return np.ascontiguousarray(words), np.ascontiguousarray(byte.astype(np.uint8).reshape(k // 512, 16, n))


def unpack_weight(words, scales, fmt):
    g, _, n = scales.shape
    words = np.ascontiguousarray(words).reshape(g, 128, n, -1)
    if fmt == "e4m3":
        vals = words.view(ml_dtypes.float8_e4m3fn).astype(np.float64)
    else:
        nib = np.empty((g, 128, n, 4), np.uint8)
        nib[..., 0::2] = words & 0xF
        nib[..., 1::2] = words >> 4
        vals = E2M1[nib]
    vals = vals * np.repeat(np.exp2(scales.astype(np.float64) - 127.0), 8, axis=1)[..., None]
    return vals.transpose(0, 1, 3, 2).reshape(g * 512, n)


def gelu(v):
    return 0.5 * v * (1.0 + np.tanh(np.sqrt(2.0 / np.pi) * (v + 0.044715 * v**3)))


T, S, K, H, T3, S2, P = 4096, 1024, 1024, 512, 2048, 1024, 512

def setup_inputs():
    n = np.random.standard_normal
    s = mx_kscale(K)[:, None]
    u = mx_kscale(H)[:, None]
    d = {}
    d["tab_words"], d["tab_scales"] = pack_weight(n((K, T)) * s, "e4m3")
    d["offs"] = striped(np.random.permutation(T)[:S])
    d["tab2_words"], d["tab2_scales"] = pack_weight(n((H, T3)) / u / H ** 0.5, "e4m3")
    d["offs2"] = striped(np.random.permutation(T3)[:S2])
    d["pos1"] = striped(np.random.permutation(S)[:P])
    d["pos2"] = striped(np.random.permutation(S)[:P])
    d["w1"] = (1.5 * n((K, H)) / s * u.T / K ** 0.5).astype(np.float32)
    d["w2_words"], d["w2_scales"] = pack_weight(1.5 * n((K, H)) / s * u.T / K ** 0.5, "e2m1")
    d["w3"] = (2.0 * n((K, H)) / s / K ** 0.5).astype(np.float32)
    d["b3"] = (0.8 * n(H)).astype(np.float32)
    d["prev"] = (0.8 * n(S2)).astype(np.float32)
    return d

def reference(tab_words, tab_scales, offs, tab2_words, tab2_scales, offs2, pos1, pos2, w1, w2_words, w2_scales, w3, b3, prev):
    v = unpack_weight(tab_words, tab_scales, "e4m3")[:, unstriped(offs)]
    v2 = unpack_weight(tab2_words, tab2_scales, "e4m3")[:, unstriped(offs2)]
    w2 = unpack_weight(w2_words, w2_scales, "e2m1")
    a = mxq(f64(w1), 0, "e4m3").T @ v
    b = w2.T @ v
    q = mxq(f64(w3), 0, "e4m3").T @ v
    trust = 1.0 / (1.0 + np.exp(-(q + f64(b3)[:, None])))
    h = np.maximum(a, b) * trust
    e = v2.T @ mxq(h, 0, "e4m3")
    first = e[:, unstriped(pos1)] + f64(prev)[:, None]
    return np.maximum(first, e[:, unstriped(pos2)])

@@ -1,0 +1,238 @@
+from contextlib import ExitStack
+
+import concourse.mybir as mybir
+
+T, S, K, H, T3, S2, NP = 4096, 1024, 1024, 512, 2048, 1024, 512
+FLOPS = 2 * (3 * K * H * S + H * S2 * S)
+
+F32 = mybir.dt.float32
+BF16 = mybir.dt.bfloat16
+I32 = mybir.dt.int32
+U32 = mybir.dt.uint32
+U16 = mybir.dt.uint16
+U8 = mybir.dt.uint8
+FP8X4 = mybir.dt.float8_e4m3fn_x4
+FP4X4 = mybir.dt.float4_e2m1fn_x4
+ALU = mybir.AluOpType
+ACT = mybir.ActivationFunctionType
+
+P = 128
+PACK = 4
+PASSES = 2
+HALF = 512
+V2_ROW = 8
+
+
+def tile_list_hotline_substance_ranking_kernel(
+    tc, tab_words, tab_scales, offs, tab2_words, tab2_scales, offs2, pos1, pos2,
+    w1, w2_words, w2_scales, w3, b3, prev, out,
+):
+    nc = tc.nc
+    with ExitStack() as ctx:
+        lists = ctx.enter_context(tc.tile_pool(name="lists", bufs=1))
+        keep = ctx.enter_context(tc.tile_pool(name="keep", bufs=1))
+        ring = ctx.enter_context(tc.tile_pool(name="ring", bufs=3))
+        psum = ctx.enter_context(tc.psum_pool(name="psum", bufs=1))
+
+        def kept(name, shape, dtype, tag=""):
+            return keep.tile(shape, dtype, name=name, align_bytes=64, tag=tag)
+
+        def bank(i):
+            return psum.tile([P, HALF], F32, name="bank%d" % i)
+
+        notes = lists.tile([P, S // 16], U16, name="notes")
+        cands = lists.tile([P, S2 // 16], U16, name="cands")
+        first = lists.tile([P, NP // 16], U16, name="first")
+        follow = lists.tile([P, NP // 16], U16, name="follow")
+
+        tab_sc = kept("tab_sc", [P, T], U8, tag="first_window")
+        w2_sc_raw = kept("w2_sc_raw", [P, PASSES, H], U8)
+        tab2_sc = kept("tab2_sc", [P, T3], U8)
+        v_sc1 = kept("v_sc1", [P, S], U8)
+        nc.vector.memset(tab_sc[:].bitcast(I32), 0)
+        nc.vector.memset(w2_sc_raw[:].rearrange("p a c -> p (a c)").bitcast(I32), 0)
+        nc.vector.memset(tab2_sc[:].bitcast(I32), 0)
+        nc.vector.memset(v_sc1[:].bitcast(I32), 0)
+
+        tab_w = [kept("tab_w%d" % a, [P, T], I32, tag="tab_w%d" % a) for a in range(PASSES)]
+        tab2_w = kept("tab2_w", [P, T3], I32)
+        w2_raw = kept("w2_raw", [P, PASSES, 2 * H], U8)
+        bias = kept("bias", [P, PACK], F32)
+        offset = kept("offset", [P, S2 // P], F32)
+        raw = {}
+        for name in ("w1", "w3"):
+            for a in range(PASSES):
+                raw[name, a] = kept("%s_raw%d" % (name, a), [P, PACK, H], F32)
+
+        def words(table, a):
+            return table[a].rearrange("p t i -> p (t i)").bitcast(I32)
+
+        def load_weight(name, w, a):
+            nc.sync.dma_start(raw[name, a][:], w[a * 512 : (a + 1) * 512, :].rearrange("(p i) c -> p i c", i=PACK))
+
+        nc.sync.dma_start(notes[:], offs)
+        nc.scalar.dma_start(w2_raw[:].bitcast(I32), w2_words.rearrange("a p c -> p a c").bitcast(I32))
+        nc.sync.dma_start(tab_w[0][:], words(tab_words, 0))
+        for q in range(4):
+            nc.gpsimd.dma_start(tab_sc[32 * q : 32 * q + 8, :].bitcast(I32), tab_scales[:, 4 * q : 4 * q + 4, :].bitcast(I32))
+        for q in range(4):
+            nc.scalar.dma_start(
+                w2_sc_raw[32 * q : 32 * q + 4].bitcast(I32),
+                w2_scales[:, 4 * q : 4 * q + 4, :].rearrange("a r c -> r a c").bitcast(I32),
+            )
+        for q in range(4):
+            nc.scalar.dma_start(
+                tab2_sc[32 * q + V2_ROW : 32 * q + V2_ROW + 4, :].bitcast(I32),
+                tab2_scales[0, 4 * q : 4 * q + 4, :].bitcast(I32),
+            )
+        nc.scalar.dma_start(bias[:], b3.rearrange("(p t) -> p t", t=PACK))
+        nc.sync.dma_start(tab_w[1][:], words(tab_words, 1))
+        nc.sync.dma_start(cands[:], offs2)
+        load_weight("w1", w1, 0)
+        load_weight("w1", w1, 1)
+        load_weight("w3", w3, 0)
+        load_weight("w3", w3, 1)
+        nc.sync.dma_start(tab2_w[:], words(tab2_words, 0))
+        nc.sync.dma_start(first[:], pos1)
+        nc.sync.dma_start(follow[:], pos2)
+        with nc.allow_non_contiguous_dma(reason="one offset a partition"):
+            nc.sync.dma_start(offset[:], prev.rearrange("(c p) -> p c", p=P))
+
+        warm = kept("warm", [P, 1], F32)
+        nc.scalar.activation(warm[:], bias[:, 0:1], ACT.Sigmoid)
+
+        w2_w = kept("w2_w", [P, PASSES, 2 * H], U8)
+        w2_sc = kept("w2_sc", [P, PASSES, H], U8)
+        for a in range(PASSES):
+            nc.vector.tensor_copy(
+                w2_w[:, a, :].bitcast(U16).rearrange("p (t m) -> p m t", t=PACK),
+                w2_raw[:, a, :].bitcast(U16).rearrange("p (m t) -> p m t", t=PACK),
+            )
+        nc.vector.tensor_copy(
+            w2_sc[:].rearrange("p a (t m) -> p a m t", t=PACK),
+            w2_sc_raw[:].rearrange("p a (m t) -> p a m t", t=PACK),
+        )
+
+        v_sc = kept("v_sc", [P, S], U8)
+        nc.vector.tensor_copy(v_sc[:], tab_sc[:].indirect(notes[:]))
+        nc.scalar.dma_start(v_sc1[0:100, :].bitcast(I32), v_sc[4:104, :].bitcast(I32))
+        v_planes = [v_sc, v_sc1]
+        v_w = {}
+
+        def gather_v(a):
+            both = kept("v_w%d" % a, [P, S], U32, tag="first_window" if a == 0 else "")
+            for jh in range(2):
+                v_w[a, jh] = both[:, jh * HALF : (jh + 1) * HALF]
+                nc.vector.tensor_copy(v_w[a, jh], tab_w[a][:].bitcast(U32).indirect(notes[:, 32 * jh : 32 * (jh + 1)]))
+
+        gather_v(0)
+        v2_sc = kept("v2_sc", [P, S2], U8, tag="tab_w0")
+        nc.vector.tensor_copy(v2_sc[:], tab2_sc[:].indirect(cands[:]))
+        gather_v(1)
+
+        groups = [(jh, t) for jh in range(2) for t in range(PACK)]
+
+        def product_pass(banks, a, stationary):
+            for g, (jh, t) in enumerate(groups):
+                lhs, lhs_sc = stationary(a, t)
+                nc.tensor.matmul_mx(
+                    banks[g][:], lhsT=lhs, lhsT_scale=lhs_sc,
+                    rhs=v_w[a, jh].bitcast(FP8X4), rhs_scale=v_planes[a][:, jh * HALF : (jh + 1) * HALF],
+                    start=(a == 0), stop=(a == PASSES - 1),
+                )
+
+        codes, planes = {}, {}
+
+        def round_weight(name, a, shares):
+            grouped = ring.tile([P, PACK * H], BF16, name="grouped", bufs=2, align_bytes=64)
+            dst = grouped[:].rearrange("p (t m i) -> p m i t", t=PACK, i=PACK)
+            src = raw[name, a][:].rearrange("p i (m t) -> p m i t", t=PACK)
+            for copy, m0, m1 in shares:
+                copy(dst[:, m0:m1], src[:, m0:m1])
+            codes[name, a] = kept("%s_codes%d" % (name, a), [P, H], U32)
+            planes[name, a] = kept("%s_plane%d" % (name, a), [P, H], U8)
+            nc.vector.quantize_mx(codes[name, a][:].bitcast(FP8X4), planes[name, a][:], grouped[:])
+
+        def fp8_weight(name):
+            return lambda a, t: (
+                codes[name, a][:, t * P : (t + 1) * P].bitcast(FP8X4),
+                planes[name, a][:, t * P : (t + 1) * P],
+            )
+
+        def fp4_weight(a, t):
+            return w2_w[:, a, 2 * t * P : 2 * (t + 1) * P].bitcast(FP4X4), w2_sc[:, a, t * P : (t + 1) * P]
+
+        banks = [bank(g) for g in range(8)]
+        for a in range(PASSES):
+            product_pass(banks, a, fp4_weight)
+        second = [kept("second%d" % g, [P, HALF], F32) for g in range(8)]
+        for g in range(8):
+            nc.scalar.copy(second[g][:], banks[g][:])
+
+        banks = [bank(g) for g in range(8)]
+        for a in range(PASSES):
+            round_weight("w1", a, [(nc.vector.tensor_copy, 0, P)])
+            product_pass(banks, a, fp8_weight("w1"))
+        larger = [kept("larger%d" % jh, [P, PACK, HALF], F32) for jh in range(2)]
+        round_weight("w3", 0, [(nc.scalar.copy, 0, P)])
+        round_weight("w3", 1, [(nc.scalar.copy, 0, P // 2), (nc.vector.tensor_copy, P // 2, P)])
+        for g, (jh, t) in enumerate(groups):
+            nc.vector.tensor_tensor(larger[jh][:, t, :], banks[g][:], second[g][:], ALU.max)
+
+        banks = [bank(g) for g in range(8)]
+        for a in range(PASSES):
+            product_pass(banks, a, fp8_weight("w3"))
+
+        v2_w = [kept("v2_w%d" % i, [P, 256], U32) for i in range(4)]
+
+        def gather_v2(i):
+            nc.vector.tensor_copy(v2_w[i][:], tab2_w[:].bitcast(U32).indirect(cands[:, 16 * i : 16 * (i + 1)]))
+
+        gather_v2(0)
+        h_w = [kept("h_w%d" % jh, [P, HALF], U32) for jh in range(2)]
+        h_sc = [kept("h_sc%d" % jh, [P, HALF], U8) for jh in range(2)]
+        for jh, j0, width in ((0, 0, 512), (1, 0, 256), (1, 256, 256)):
+            trust = kept("trust%d_%d" % (jh, j0), [P, PACK, width], F32)
+            for t in range(PACK):
+                nc.scalar.activation(
+                    trust[:, t, :], banks[PACK * jh + t][:, j0 : j0 + width], ACT.Sigmoid, bias=bias[:, t : t + 1]
+                )
+            h = kept("h%d_%d" % (jh, j0), [P, PACK * width], BF16)
+            nc.vector.tensor_tensor(
+                h[:].rearrange("p (c i t) -> p c t i", i=4, t=PACK),
+                larger[jh][:, :, j0 : j0 + width].rearrange("p t (c i) -> p c t i", i=4),
+                trust[:].rearrange("p t (c i) -> p c t i", i=4),
+                ALU.mult,
+            )
+            nc.vector.quantize_mx(h_w[jh][:, j0 : j0 + width].bitcast(FP8X4), h_sc[jh][:, j0 : j0 + width], h[:])
+        for i in range(1, 4):
+            gather_v2(i)
+
+        picked = {}
+
+        def finish(c):
+            at_first, at_follow = picked[c]
+            result = ring.tile([P, NP], F32, name="result")
+            nc.vector.scalar_tensor_tensor(result[:], at_first[:], offset[:, c : c + 1], at_follow[:], ALU.add, ALU.max)
+            nc.sync.dma_start(out[c * P : (c + 1) * P, :], result[:])
+
+        for c in range(S2 // P):
+            scores = ring.tile([P, S], F32, name="scores", bufs=4)
+            for jh in range(2):
+                acc = bank(PACK * jh + c % PACK)
+                nc.tensor.matmul_mx(
+                    acc[:],
+                    lhsT=v2_w[c // 2][:, (c % 2) * P : (c % 2 + 1) * P].bitcast(FP8X4),
+                    lhsT_scale=v2_sc[V2_ROW:P, c * P : (c + 1) * P],
+                    rhs=h_w[jh][:].bitcast(FP8X4), rhs_scale=h_sc[jh][:],
+                    start=True, stop=True,
+                )
+                nc.scalar.copy(scores[:, jh * HALF : (jh + 1) * HALF], acc[:])
+            at_first = ring.tile([P, NP], F32, name="at_first")
+            at_follow = ring.tile([P, NP], F32, name="at_follow")
+            nc.vector.tensor_copy(at_first[:], scores[:].indirect(first[:]))
+            nc.vector.tensor_copy(at_follow[:], scores[:].indirect(follow[:]))
+            picked[c] = (at_first, at_follow)
+            if c > 0:
+                finish(c - 1)
+        finish(S2 // P - 1)

@@ -45,17 +45,21 @@ def tile_list_hotline_substance_ranking_kernel(
         first = lists.tile([P, NP // 16], U16, name="first")
         follow = lists.tile([P, NP // 16], U16, name="follow")
 
-        tab_sc = kept("tab_sc", [P, T], U8, tag="first_window")
-        w2_sc_raw = kept("w2_sc_raw", [P, PASSES, H], U8)
         tab2_sc = kept("tab2_sc", [P, T3], U8)
+        w2_sc_raw = kept("w2_sc_raw", [P, PASSES, H], U8, tag="w2_sc_raw")
+        tab_sc = kept("tab_sc", [P, T], U8)
         v_sc1 = kept("v_sc1", [P, S], U8)
-        nc.vector.memset(tab_sc[:].bitcast(I32), 0)
-        nc.vector.memset(w2_sc_raw[:].rearrange("p a c -> p (a c)").bitcast(I32), 0)
+        nc.gpsimd.memset(tab_sc[:, 0:2560].bitcast(I32), 0)
+        nc.vector.memset(tab_sc[:, 2560:T].bitcast(I32), 0)
         nc.vector.memset(tab2_sc[:].bitcast(I32), 0)
+        nc.vector.memset(w2_sc_raw[:].rearrange("p a c -> p (a c)").bitcast(I32), 0)
+        warm = kept("warm", [P, 2], F32)
+        nc.gpsimd.memset(warm[:, 0:1], 0.0)
+        nc.scalar.activation(warm[:, 1:2], warm[:, 0:1], ACT.Sigmoid)
         nc.vector.memset(v_sc1[:].bitcast(I32), 0)
 
-        tab_w = [kept("tab_w%d" % a, [P, T], I32, tag="tab_w%d" % a) for a in range(PASSES)]
-        tab2_w = kept("tab2_w", [P, T3], I32)
+        tab_w = [kept("tab_w%d" % a, [P, T], I32) for a in range(PASSES)]
+        tab2_w = kept("tab2_w", [P, T3], I32, tag="tab2_w")
         w2_raw = kept("w2_raw", [P, PASSES, 2 * H], U8)
         bias = kept("bias", [P, PACK], F32)
         offset = kept("offset", [P, S2 // P], F32)
@@ -70,88 +74,107 @@ def tile_list_hotline_substance_ranking_kernel(
         def load_weight(name, w, a):
             nc.sync.dma_start(raw[name, a][:], w[a * 512 : (a + 1) * 512, :].rearrange("(p i) c -> p i c", i=PACK))
 
-        nc.sync.dma_start(notes[:], offs)
-        nc.scalar.dma_start(w2_raw[:].bitcast(I32), w2_words.rearrange("a p c -> p a c").bitcast(I32))
-        nc.sync.dma_start(tab_w[0][:], words(tab_words, 0))
-        for q in range(4):
-            nc.gpsimd.dma_start(tab_sc[32 * q : 32 * q + 8, :].bitcast(I32), tab_scales[:, 4 * q : 4 * q + 4, :].bitcast(I32))
-        for q in range(4):
-            nc.scalar.dma_start(
-                w2_sc_raw[32 * q : 32 * q + 4].bitcast(I32),
-                w2_scales[:, 4 * q : 4 * q + 4, :].rearrange("a r c -> r a c").bitcast(I32),
-            )
-        for q in range(4):
-            nc.scalar.dma_start(
+        def load_tab2_scales(q):
+            nc.sync.dma_start(
                 tab2_sc[32 * q + V2_ROW : 32 * q + V2_ROW + 4, :].bitcast(I32),
                 tab2_scales[0, 4 * q : 4 * q + 4, :].bitcast(I32),
             )
-        nc.scalar.dma_start(bias[:], b3.rearrange("(p t) -> p t", t=PACK))
-        nc.sync.dma_start(tab_w[1][:], words(tab_words, 1))
+
+        def load_w2_scales(q):
+            nc.sync.dma_start(
+                w2_sc_raw[32 * q : 32 * q + 4].bitcast(I32),
+                w2_scales[:, 4 * q : 4 * q + 4, :].rearrange("a r c -> r a c").bitcast(I32),
+            )
+
         nc.sync.dma_start(cands[:], offs2)
+        nc.sync.dma_start(notes[:], offs)
+        nc.sync.dma_start(first[:], pos1)
+        nc.sync.dma_start(follow[:], pos2)
+        nc.sync.dma_start(bias[:], b3.rearrange("(p t) -> p t", t=PACK))
+        nc.sync.dma_start(w2_raw[:].bitcast(I32), w2_words.rearrange("a p c -> p a c").bitcast(I32))
+        nc.sync.dma_start(tab_w[0][:, 0 : T // 2], words(tab_words, 0)[:, 0 : T // 2])
+        for r in range(4):
+            nc.sync.dma_start(
+                tab_sc[r:P:16, :].bitcast(I32), tab_scales.rearrange("a (q r) c -> r q a c", r=4)[r].bitcast(I32)
+            )
+        load_tab2_scales(0)
+        load_tab2_scales(1)
+        nc.sync.dma_start(tab_w[0][:, T // 2 : T], words(tab_words, 0)[:, T // 2 : T])
+        load_tab2_scales(2)
+        load_tab2_scales(3)
+        for q in range(4):
+            load_w2_scales(q)
+        nc.sync.dma_start(tab_w[1][:], words(tab_words, 1))
+
+        w2_w = kept("w2_w", [P, PASSES, 2 * H], U8)
+        w2_sc = kept("w2_sc", [P, PASSES, H], U8)
+        nc.vector.tensor_copy(
+            w2_w[:].bitcast(U16).rearrange("p a (t m) -> p a t m", t=PACK),
+            w2_raw[:].bitcast(U16).rearrange("p a (m t) -> p a t m", t=PACK),
+        )
+        v_sc = kept("v_sc", [P, S], U8)
+        nc.vector.tensor_copy(v_sc[:], tab_sc[:].indirect(notes[:]))
+        nc.sync.dma_start(v_sc1[0:100, :].bitcast(I32), v_sc[16:116, :].bitcast(I32))
         load_weight("w1", w1, 0)
         load_weight("w1", w1, 1)
         load_weight("w3", w3, 0)
         load_weight("w3", w3, 1)
         nc.sync.dma_start(tab2_w[:], words(tab2_words, 0))
-        nc.sync.dma_start(first[:], pos1)
-        nc.sync.dma_start(follow[:], pos2)
         with nc.allow_non_contiguous_dma(reason="one offset a partition"):
             nc.sync.dma_start(offset[:], prev.rearrange("(c p) -> p c", p=P))
 
-        warm = kept("warm", [P, 1], F32)
-        nc.scalar.activation(warm[:], bias[:, 0:1], ACT.Sigmoid)
-
-        w2_w = kept("w2_w", [P, PASSES, 2 * H], U8)
-        w2_sc = kept("w2_sc", [P, PASSES, H], U8)
-        for a in range(PASSES):
-            nc.vector.tensor_copy(
-                w2_w[:, a, :].bitcast(U16).rearrange("p (t m) -> p m t", t=PACK),
-                w2_raw[:, a, :].bitcast(U16).rearrange("p (m t) -> p m t", t=PACK),
-            )
-        nc.vector.tensor_copy(
-            w2_sc[:].rearrange("p a (t m) -> p a m t", t=PACK),
-            w2_sc_raw[:].rearrange("p a (m t) -> p a m t", t=PACK),
-        )
-
-        v_sc = kept("v_sc", [P, S], U8)
-        nc.vector.tensor_copy(v_sc[:], tab_sc[:].indirect(notes[:]))
-        nc.scalar.dma_start(v_sc1[0:100, :].bitcast(I32), v_sc[4:104, :].bitcast(I32))
         v_planes = [v_sc, v_sc1]
         v_w = {}
 
         def gather_v(a):
-            both = kept("v_w%d" % a, [P, S], U32, tag="first_window" if a == 0 else "")
             for jh in range(2):
-                v_w[a, jh] = both[:, jh * HALF : (jh + 1) * HALF]
-                nc.vector.tensor_copy(v_w[a, jh], tab_w[a][:].bitcast(U32).indirect(notes[:, 32 * jh : 32 * (jh + 1)]))
+                v_w[a, jh] = kept("v_w%d%d" % (a, jh), [P, HALF], U32)
+                nc.vector.tensor_copy(v_w[a, jh][:], tab_w[a][:].bitcast(U32).indirect(notes[:, 32 * jh : 32 * (jh + 1)]))
 
         gather_v(0)
-        v2_sc = kept("v2_sc", [P, S2], U8, tag="tab_w0")
-        nc.vector.tensor_copy(v2_sc[:], tab2_sc[:].indirect(cands[:]))
+        nc.vector.tensor_copy(
+            w2_sc[:].rearrange("p a (t m) -> p a t m", t=PACK),
+            w2_sc_raw[:].rearrange("p a (m t) -> p a t m", t=PACK),
+        )
+        v2_sc = {}
+
+        def gather_v2_scales(i, tag):
+            v2_sc[i] = kept("v2_sc%d" % i, [P, HALF], U8, tag=tag)
+            nc.vector.tensor_copy(v2_sc[i][:], tab2_sc[:].indirect(cands[:, 32 * i : 32 * (i + 1)]))
+
+        gather_v2_scales(0, "w2_sc_raw")
         gather_v(1)
 
         groups = [(jh, t) for jh in range(2) for t in range(PACK)]
 
-        def product_pass(banks, a, stationary):
-            for g, (jh, t) in enumerate(groups):
+        def product(banks, order, stationary):
+            for g, a in order:
+                jh, t = groups[g]
                 lhs, lhs_sc = stationary(a, t)
                 nc.tensor.matmul_mx(
                     banks[g][:], lhsT=lhs, lhsT_scale=lhs_sc,
-                    rhs=v_w[a, jh].bitcast(FP8X4), rhs_scale=v_planes[a][:, jh * HALF : (jh + 1) * HALF],
+                    rhs=v_w[a, jh][:].bitcast(FP8X4), rhs_scale=v_planes[a][:, jh * HALF : (jh + 1) * HALF],
                     start=(a == 0), stop=(a == PASSES - 1),
                 )
 
-        codes, planes = {}, {}
+        by_pass = [(g, a) for a in range(PASSES) for g in range(8)]
+        by_group = [(g, a) for g in range(8) for a in range(PASSES)]
+        codes, planes, rounded = {}, {}, {}
+
+        def pool_round(dst, src):
+            nc.gpsimd.tensor_scalar(dst, src, 1.0, 0.0, ALU.mult, ALU.add)
 
         def round_weight(name, a, shares):
-            grouped = ring.tile([P, PACK * H], BF16, name="grouped", bufs=2, align_bytes=64)
-            dst = grouped[:].rearrange("p (t m i) -> p m i t", t=PACK, i=PACK)
-            src = raw[name, a][:].rearrange("p i (m t) -> p m i t", t=PACK)
+            rounded[name, a] = ring.tile([P, PACK * H], BF16, name="grouped", bufs=2, align_bytes=64)
+            dst = rounded[name, a][:].rearrange("p (t m i) -> p m t i", t=PACK, i=PACK)
+            src = raw[name, a][:].rearrange("p i (m t) -> p m t i", t=PACK)
             for copy, m0, m1 in shares:
                 copy(dst[:, m0:m1], src[:, m0:m1])
+
+        def quantize_weight(name, a):
             codes[name, a] = kept("%s_codes%d" % (name, a), [P, H], U32)
             planes[name, a] = kept("%s_plane%d" % (name, a), [P, H], U8)
-            nc.vector.quantize_mx(codes[name, a][:].bitcast(FP8X4), planes[name, a][:], grouped[:])
+            nc.vector.quantize_mx(codes[name, a][:].bitcast(FP8X4), planes[name, a][:], rounded[name, a][:])
 
         def fp8_weight(name):
             return lambda a, t: (
@@ -162,42 +185,44 @@ def tile_list_hotline_substance_ranking_kernel(
         def fp4_weight(a, t):
             return w2_w[:, a, 2 * t * P : 2 * (t + 1) * P].bitcast(FP4X4), w2_sc[:, a, t * P : (t + 1) * P]
 
+        round_weight("w1", 0, [(nc.vector.tensor_copy, 0, 128)])
+        quantize_weight("w1", 0)
+        round_weight("w1", 1, [(nc.vector.tensor_copy, 0, 128)])
+        quantize_weight("w1", 1)
         banks = [bank(g) for g in range(8)]
-        for a in range(PASSES):
-            product_pass(banks, a, fp4_weight)
+        product(banks, by_pass, fp4_weight)
         second = [kept("second%d" % g, [P, HALF], F32) for g in range(8)]
         for g in range(8):
             nc.scalar.copy(second[g][:], banks[g][:])
 
         banks = [bank(g) for g in range(8)]
-        for a in range(PASSES):
-            round_weight("w1", a, [(nc.vector.tensor_copy, 0, P)])
-            product_pass(banks, a, fp8_weight("w1"))
+        product(banks, by_group, fp8_weight("w1"))
         larger = [kept("larger%d" % jh, [P, PACK, HALF], F32) for jh in range(2)]
-        round_weight("w3", 0, [(nc.scalar.copy, 0, P)])
-        round_weight("w3", 1, [(nc.scalar.copy, 0, P // 2), (nc.vector.tensor_copy, P // 2, P)])
+        for a, shares in ((0, [(nc.scalar.copy, 0, 128)]), (1, [(nc.scalar.copy, 0, 128)])):
+            round_weight("w3", a, shares)
+            quantize_weight("w3", a)
         for g, (jh, t) in enumerate(groups):
             nc.vector.tensor_tensor(larger[jh][:, t, :], banks[g][:], second[g][:], ALU.max)
 
         banks = [bank(g) for g in range(8)]
-        for a in range(PASSES):
-            product_pass(banks, a, fp8_weight("w3"))
+        product(banks, by_group, fp8_weight("w3"))
+        v2_w = {}
 
-        v2_w = [kept("v2_w%d" % i, [P, 256], U32) for i in range(4)]
+        def gather_v2(i, tag):
+            v2_w[i] = kept("v2_w%d" % i, [P, HALF], U32, tag=tag)
+            nc.vector.tensor_copy(v2_w[i][:], tab2_w[:].bitcast(U32).indirect(cands[:, 32 * i : 32 * (i + 1)]))
 
-        def gather_v2(i):
-            nc.vector.tensor_copy(v2_w[i][:], tab2_w[:].bitcast(U32).indirect(cands[:, 16 * i : 16 * (i + 1)]))
+        gather_v2(0, "")
 
-        gather_v2(0)
         h_w = [kept("h_w%d" % jh, [P, HALF], U32) for jh in range(2)]
         h_sc = [kept("h_sc%d" % jh, [P, HALF], U8) for jh in range(2)]
-        for jh, j0, width in ((0, 0, 512), (1, 0, 256), (1, 256, 256)):
+        for jh, j0, width in ((0, 0, 512), (1, 0, 512)):
             trust = kept("trust%d_%d" % (jh, j0), [P, PACK, width], F32)
             for t in range(PACK):
                 nc.scalar.activation(
                     trust[:, t, :], banks[PACK * jh + t][:, j0 : j0 + width], ACT.Sigmoid, bias=bias[:, t : t + 1]
                 )
-            h = kept("h%d_%d" % (jh, j0), [P, PACK * width], BF16)
+            h = kept("h%d_%d" % (jh, j0), [P, PACK * width], BF16, tag="h%d" % jh)
             nc.vector.tensor_tensor(
                 h[:].rearrange("p (c i t) -> p c t i", i=4, t=PACK),
                 larger[jh][:, :, j0 : j0 + width].rearrange("p t (c i) -> p c t i", i=4),
@@ -205,9 +230,9 @@ def tile_list_hotline_substance_ranking_kernel(
                 ALU.mult,
             )
             nc.vector.quantize_mx(h_w[jh][:, j0 : j0 + width].bitcast(FP8X4), h_sc[jh][:, j0 : j0 + width], h[:])
-        for i in range(1, 4):
-            gather_v2(i)
 
+        gather_v2(1, "h1")
+        gather_v2_scales(1, "tab2_w")
         picked = {}
 
         def finish(c):
@@ -222,8 +247,8 @@ def tile_list_hotline_substance_ranking_kernel(
                 acc = bank(PACK * jh + c % PACK)
                 nc.tensor.matmul_mx(
                     acc[:],
-                    lhsT=v2_w[c // 2][:, (c % 2) * P : (c % 2 + 1) * P].bitcast(FP8X4),
-                    lhsT_scale=v2_sc[V2_ROW:P, c * P : (c + 1) * P],
+                    lhsT=v2_w[c // 4][:, (c % 4) * P : (c % 4 + 1) * P].bitcast(FP8X4),
+                    lhsT_scale=v2_sc[c // 4][V2_ROW:P, (c % 4) * P : (c % 4 + 1) * P],
                     rhs=h_w[jh][:].bitcast(FP8X4), rhs_scale=h_sc[jh][:],
                     start=True, stop=True,
                 )

from contextlib import ExitStack

import concourse.mybir as mybir

T, S, K, H, T3, S2, NP = 4096, 1024, 1024, 512, 2048, 1024, 512
FLOPS = 2 * (3 * K * H * S + H * S2 * S)

F32 = mybir.dt.float32
BF16 = mybir.dt.bfloat16
I32 = mybir.dt.int32
U32 = mybir.dt.uint32
U16 = mybir.dt.uint16
U8 = mybir.dt.uint8
FP8X4 = mybir.dt.float8_e4m3fn_x4
FP4X4 = mybir.dt.float4_e2m1fn_x4
ALU = mybir.AluOpType
ACT = mybir.ActivationFunctionType

P = 128
PACK = 4
PASSES = 2
HALF = 512
V2_ROW = 8


def tile_list_hotline_substance_ranking_kernel(
    tc, tab_words, tab_scales, offs, tab2_words, tab2_scales, offs2, pos1, pos2,
    w1, w2_words, w2_scales, w3, b3, prev, out,
):
    nc = tc.nc
    with ExitStack() as ctx:
        lists = ctx.enter_context(tc.tile_pool(name="lists", bufs=1))
        keep = ctx.enter_context(tc.tile_pool(name="keep", bufs=1))
        ring = ctx.enter_context(tc.tile_pool(name="ring", bufs=3))
        psum = ctx.enter_context(tc.psum_pool(name="psum", bufs=1))

        def kept(name, shape, dtype, tag=""):
            return keep.tile(shape, dtype, name=name, align_bytes=64, tag=tag)

        def bank(i):
            return psum.tile([P, HALF], F32, name="bank%d" % i)

        notes = lists.tile([P, S // 16], U16, name="notes")
        cands = lists.tile([P, S2 // 16], U16, name="cands")
        first = lists.tile([P, NP // 16], U16, name="first")
        follow = lists.tile([P, NP // 16], U16, name="follow")

        tab2_sc = kept("tab2_sc", [P, T3], U8)
        w2_sc_raw = kept("w2_sc_raw", [P, PASSES, H], U8, tag="w2_sc_raw")
        tab_sc = kept("tab_sc", [P, T], U8)
        v_sc1 = kept("v_sc1", [P, S], U8)
        nc.gpsimd.memset(tab_sc[:, 0:2560].bitcast(I32), 0)
        nc.vector.memset(tab_sc[:, 2560:T].bitcast(I32), 0)
        nc.vector.memset(tab2_sc[:].bitcast(I32), 0)
        nc.vector.memset(w2_sc_raw[:].rearrange("p a c -> p (a c)").bitcast(I32), 0)
        warm = kept("warm", [P, 2], F32)
        nc.gpsimd.memset(warm[:, 0:1], 0.0)
        nc.scalar.activation(warm[:, 1:2], warm[:, 0:1], ACT.Sigmoid)
        nc.vector.memset(v_sc1[:].bitcast(I32), 0)

        tab_w = [kept("tab_w%d" % a, [P, T], I32) for a in range(PASSES)]
        tab2_w = kept("tab2_w", [P, T3], I32, tag="tab2_w")
        w2_raw = kept("w2_raw", [P, PASSES, 2 * H], U8)
        bias = kept("bias", [P, PACK], F32)
        offset = kept("offset", [P, S2 // P], F32)
        raw = {}
        for name in ("w1", "w3"):
            for a in range(PASSES):
                raw[name, a] = kept("%s_raw%d" % (name, a), [P, PACK, H], F32)

        def words(table, a):
            return table[a].rearrange("p t i -> p (t i)").bitcast(I32)

        def load_weight(name, w, a):
            nc.sync.dma_start(raw[name, a][:], w[a * 512 : (a + 1) * 512, :].rearrange("(p i) c -> p i c", i=PACK))

        def load_tab2_scales(q):
            nc.sync.dma_start(
                tab2_sc[32 * q + V2_ROW : 32 * q + V2_ROW + 4, :].bitcast(I32),
                tab2_scales[0, 4 * q : 4 * q + 4, :].bitcast(I32),
            )

        def load_w2_scales(q):
            nc.sync.dma_start(
                w2_sc_raw[32 * q : 32 * q + 4].bitcast(I32),
                w2_scales[:, 4 * q : 4 * q + 4, :].rearrange("a r c -> r a c").bitcast(I32),
            )

        nc.sync.dma_start(cands[:], offs2)
        nc.sync.dma_start(notes[:], offs)
        nc.sync.dma_start(first[:], pos1)
        nc.sync.dma_start(follow[:], pos2)
        nc.sync.dma_start(bias[:], b3.rearrange("(p t) -> p t", t=PACK))
        nc.sync.dma_start(w2_raw[:].bitcast(I32), w2_words.rearrange("a p c -> p a c").bitcast(I32))
        nc.sync.dma_start(tab_w[0][:, 0 : T // 2], words(tab_words, 0)[:, 0 : T // 2])
        for r in range(4):
            nc.sync.dma_start(
                tab_sc[r:P:16, :].bitcast(I32), tab_scales.rearrange("a (q r) c -> r q a c", r=4)[r].bitcast(I32)
            )
        load_tab2_scales(0)
        load_tab2_scales(1)
        nc.sync.dma_start(tab_w[0][:, T // 2 : T], words(tab_words, 0)[:, T // 2 : T])
        load_tab2_scales(2)
        load_tab2_scales(3)
        for q in range(4):
            load_w2_scales(q)
        nc.sync.dma_start(tab_w[1][:], words(tab_words, 1))

        w2_w = kept("w2_w", [P, PASSES, 2 * H], U8)
        w2_sc = kept("w2_sc", [P, PASSES, H], U8)
        nc.vector.tensor_copy(
            w2_w[:].bitcast(U16).rearrange("p a (t m) -> p a t m", t=PACK),
            w2_raw[:].bitcast(U16).rearrange("p a (m t) -> p a t m", t=PACK),
        )
        v_sc = kept("v_sc", [P, S], U8)
        nc.vector.tensor_copy(v_sc[:], tab_sc[:].indirect(notes[:]))
        nc.sync.dma_start(v_sc1[0:100, :].bitcast(I32), v_sc[16:116, :].bitcast(I32))
        load_weight("w1", w1, 0)
        load_weight("w1", w1, 1)
        load_weight("w3", w3, 0)
        load_weight("w3", w3, 1)
        nc.sync.dma_start(tab2_w[:], words(tab2_words, 0))
        with nc.allow_non_contiguous_dma(reason="one offset a partition"):
            nc.sync.dma_start(offset[:], prev.rearrange("(c p) -> p c", p=P))

        v_planes = [v_sc, v_sc1]
        v_w = {}

        def gather_v(a):
            for jh in range(2):
                v_w[a, jh] = kept("v_w%d%d" % (a, jh), [P, HALF], U32)
                nc.vector.tensor_copy(v_w[a, jh][:], tab_w[a][:].bitcast(U32).indirect(notes[:, 32 * jh : 32 * (jh + 1)]))

        gather_v(0)
        nc.vector.tensor_copy(
            w2_sc[:].rearrange("p a (t m) -> p a t m", t=PACK),
            w2_sc_raw[:].rearrange("p a (m t) -> p a t m", t=PACK),
        )
        v2_sc = {}

        def gather_v2_scales(i, tag):
            v2_sc[i] = kept("v2_sc%d" % i, [P, HALF], U8, tag=tag)
            nc.vector.tensor_copy(v2_sc[i][:], tab2_sc[:].indirect(cands[:, 32 * i : 32 * (i + 1)]))

        gather_v2_scales(0, "w2_sc_raw")
        gather_v(1)

        groups = [(jh, t) for jh in range(2) for t in range(PACK)]

        def product(banks, order, stationary):
            for g, a in order:
                jh, t = groups[g]
                lhs, lhs_sc = stationary(a, t)
                nc.tensor.matmul_mx(
                    banks[g][:], lhsT=lhs, lhsT_scale=lhs_sc,
                    rhs=v_w[a, jh][:].bitcast(FP8X4), rhs_scale=v_planes[a][:, jh * HALF : (jh + 1) * HALF],
                    start=(a == 0), stop=(a == PASSES - 1),
                )

        by_pass = [(g, a) for a in range(PASSES) for g in range(8)]
        by_group = [(g, a) for g in range(8) for a in range(PASSES)]
        codes, planes, rounded = {}, {}, {}

        def pool_round(dst, src):
            nc.gpsimd.tensor_scalar(dst, src, 1.0, 0.0, ALU.mult, ALU.add)

        def round_weight(name, a, shares):
            rounded[name, a] = ring.tile([P, PACK * H], BF16, name="grouped", bufs=2, align_bytes=64)
            dst = rounded[name, a][:].rearrange("p (t m i) -> p m t i", t=PACK, i=PACK)
            src = raw[name, a][:].rearrange("p i (m t) -> p m t i", t=PACK)
            for copy, m0, m1 in shares:
                copy(dst[:, m0:m1], src[:, m0:m1])

        def quantize_weight(name, a):
            codes[name, a] = kept("%s_codes%d" % (name, a), [P, H], U32)
            planes[name, a] = kept("%s_plane%d" % (name, a), [P, H], U8)
            nc.vector.quantize_mx(codes[name, a][:].bitcast(FP8X4), planes[name, a][:], rounded[name, a][:])

        def fp8_weight(name):
            return lambda a, t: (
                codes[name, a][:, t * P : (t + 1) * P].bitcast(FP8X4),
                planes[name, a][:, t * P : (t + 1) * P],
            )

        def fp4_weight(a, t):
            return w2_w[:, a, 2 * t * P : 2 * (t + 1) * P].bitcast(FP4X4), w2_sc[:, a, t * P : (t + 1) * P]

        round_weight("w1", 0, [(nc.vector.tensor_copy, 0, 128)])
        quantize_weight("w1", 0)
        round_weight("w1", 1, [(nc.vector.tensor_copy, 0, 128)])
        quantize_weight("w1", 1)
        banks = [bank(g) for g in range(8)]
        product(banks, by_pass, fp4_weight)
        second = [kept("second%d" % g, [P, HALF], F32) for g in range(8)]
        for g in range(8):
            nc.scalar.copy(second[g][:], banks[g][:])

        banks = [bank(g) for g in range(8)]
        product(banks, by_group, fp8_weight("w1"))
        larger = [kept("larger%d" % jh, [P, PACK, HALF], F32) for jh in range(2)]
        for a, shares in ((0, [(nc.scalar.copy, 0, 128)]), (1, [(nc.scalar.copy, 0, 128)])):
            round_weight("w3", a, shares)
            quantize_weight("w3", a)
        for g, (jh, t) in enumerate(groups):
            nc.vector.tensor_tensor(larger[jh][:, t, :], banks[g][:], second[g][:], ALU.max)

        banks = [bank(g) for g in range(8)]
        product(banks, by_group, fp8_weight("w3"))
        v2_w = {}

        def gather_v2(i, tag):
            v2_w[i] = kept("v2_w%d" % i, [P, HALF], U32, tag=tag)
            nc.vector.tensor_copy(v2_w[i][:], tab2_w[:].bitcast(U32).indirect(cands[:, 32 * i : 32 * (i + 1)]))

        gather_v2(0, "")

        h_w = [kept("h_w%d" % jh, [P, HALF], U32) for jh in range(2)]
        h_sc = [kept("h_sc%d" % jh, [P, HALF], U8) for jh in range(2)]
        for jh, j0, width in ((0, 0, 512), (1, 0, 512)):
            trust = kept("trust%d_%d" % (jh, j0), [P, PACK, width], F32)
            for t in range(PACK):
                nc.scalar.activation(
                    trust[:, t, :], banks[PACK * jh + t][:, j0 : j0 + width], ACT.Sigmoid, bias=bias[:, t : t + 1]
                )
            h = kept("h%d_%d" % (jh, j0), [P, PACK * width], BF16, tag="h%d" % jh)
            nc.vector.tensor_tensor(
                h[:].rearrange("p (c i t) -> p c t i", i=4, t=PACK),
                larger[jh][:, :, j0 : j0 + width].rearrange("p t (c i) -> p c t i", i=4),
                trust[:].rearrange("p t (c i) -> p c t i", i=4),
                ALU.mult,
            )
            nc.vector.quantize_mx(h_w[jh][:, j0 : j0 + width].bitcast(FP8X4), h_sc[jh][:, j0 : j0 + width], h[:])

        gather_v2(1, "h1")
        gather_v2_scales(1, "tab2_w")
        picked = {}

        def finish(c):
            at_first, at_follow = picked[c]
            result = ring.tile([P, NP], F32, name="result")
            nc.vector.scalar_tensor_tensor(result[:], at_first[:], offset[:, c : c + 1], at_follow[:], ALU.add, ALU.max)
            nc.sync.dma_start(out[c * P : (c + 1) * P, :], result[:])

        for c in range(S2 // P):
            scores = ring.tile([P, S], F32, name="scores", bufs=4)
            for jh in range(2):
                acc = bank(PACK * jh + c % PACK)
                nc.tensor.matmul_mx(
                    acc[:],
                    lhsT=v2_w[c // 4][:, (c % 4) * P : (c % 4 + 1) * P].bitcast(FP8X4),
                    lhsT_scale=v2_sc[c // 4][V2_ROW:P, (c % 4) * P : (c % 4 + 1) * P],
                    rhs=h_w[jh][:].bitcast(FP8X4), rhs_scale=h_sc[jh][:],
                    start=True, stop=True,
                )
                nc.scalar.copy(scores[:, jh * HALF : (jh + 1) * HALF], acc[:])
            at_first = ring.tile([P, NP], F32, name="at_first")
            at_follow = ring.tile([P, NP], F32, name="at_follow")
            nc.vector.tensor_copy(at_first[:], scores[:].indirect(first[:]))
            nc.vector.tensor_copy(at_follow[:], scores[:].indirect(follow[:]))
            picked[c] = (at_first, at_follow)
            if c > 0:
                finish(c - 1)
        finish(S2 // P - 1)
